import numpy as np
import ml_dtypes


def mxq(x, axis, fmt="e4m3"):
    dtype, down = {"e4m3": (ml_dtypes.float8_e4m3fn, 7), "e5m2": (ml_dtypes.float8_e5m2, 14)}[fmt]
    v = np.moveaxis(np.asarray(x, np.float32).astype(ml_dtypes.bfloat16).astype(np.float64), axis, -1)
    blocks = v.reshape(v.shape[:-1] + (-1, 32))
    amax = np.abs(blocks).max(-1, keepdims=True)
    byte = np.maximum(np.where(amax > 0, np.frexp(amax)[1] - 1 + 127, 0) - down, 1)
    scale = np.exp2(byte - 127.0)
    codes = (blocks / scale).astype(np.float32).astype(dtype).astype(np.float64)
    return np.moveaxis((codes * scale).reshape(v.shape), -1, axis)


WIDE = False


def mx_kscale(k):
    if not WIDE:
        return np.ones(k)
    levels = np.array([10, -10, 5, -5, 0])
    if k % 512:
        return np.exp2(np.random.permutation(np.resize(levels, k // 32))).repeat(32)
    a = np.empty((k // 512, 16))
    for p in range(k // 512):
        a[p, :8] = np.random.permutation(np.resize(levels, 8))
        for g in range(8):
            far = levels[np.abs(levels - a[p, g]) >= 10]
            a[p, g + 8] = far[np.random.randint(len(far))]
    return np.exp2(a.ravel()).repeat(32)


def f64(x):
    return np.asarray(x).astype(np.float64)


def striped8(idx):
    return np.asarray(idx).reshape(8, -1, 16).transpose(0, 2, 1).reshape(128, -1).astype(np.uint16)


def unstriped8(offs):
    return offs.reshape(8, 16, -1).transpose(0, 2, 1).reshape(8, -1).astype(np.int64)


def pick8(x, idx, run):
    r = np.arange(len(x))
    return x[r[:, None], idx[r % (8 * run) // run]]


E2M1 = np.array([0.0, 0.5, 1.0, 1.5, 2.0, 3.0, 4.0, 6.0, -0.0, -0.5, -1.0, -1.5, -2.0, -3.0, -4.0, -6.0])


def pack_weight(w, fmt):
    k, n = w.shape
    w = f64(np.asarray(w, np.float32).astype(ml_dtypes.bfloat16)).reshape(k // 32, 32, n)
    amax = np.abs(w).max(1)
    if fmt == "e4m3":
        byte = np.frexp(amax)[1] - 1 + 127 - 7
    else:
        mant, ex = np.frexp(amax / 6.0)
        byte = np.where(mant > 0.5, ex, ex - 1) + 127
    byte = np.clip(np.where(amax > 0, byte, 1), 1, 254)
    scaled = (w * np.exp2(127.0 - byte)[:, None, :]).reshape(k, n).astype(np.float32)
    by_word = np.ascontiguousarray(scaled.reshape(k // 512, 128, 4, n).transpose(0, 1, 3, 2))
    if fmt == "e4m3":
        words = by_word.astype(ml_dtypes.float8_e4m3fn).view(np.uint8)
    else:
        c = by_word.astype(ml_dtypes.float4_e2m1fn).view(np.uint8) & 0xF
        words = (c[..., 0::2] | (c[..., 1::2] << 4)).reshape(k // 512, 128, 2 * n)
    return np.ascontiguousarray(words), np.ascontiguousarray(byte.astype(np.uint8).reshape(k // 512, 16, n))


def unpack_weight(words, scales, fmt):
    g, _, n = scales.shape
    words = np.ascontiguousarray(words).reshape(g, 128, n, -1)
    if fmt == "e4m3":
        vals = words.view(ml_dtypes.float8_e4m3fn).astype(np.float64)
    else:
        nib = np.empty((g, 128, n, 4), np.uint8)
        nib[..., 0::2] = words & 0xF
        nib[..., 1::2] = words >> 4
        vals = E2M1[nib]
    vals = vals * np.repeat(np.exp2(scales.astype(np.float64) - 127.0), 8, axis=1)[..., None]
    return vals.transpose(0, 1, 3, 2).reshape(g * 512, n)


def sigmoid(v):
    return 1.0 / (1.0 + np.exp(-v))


D, T, U, I, Q = 512, 1024, 1024, 512, 128


def setup_inputs():
    n = np.random.standard_normal
    idx = np.stack([np.random.permutation(T)[:I] for _ in range(8)])
    idx2 = np.stack([np.random.permutation(U)[:I] for _ in range(8)])
    idx3 = np.stack([np.random.permutation(T)[:I] for _ in range(8)])
    idx4 = np.stack([np.random.permutation(T)[:I] for _ in range(8)])
    fd = mx_kscale(D)
    keysp = pack_weight(n((D, T)) / fd[:, None], "e2m1")
    notesp = pack_weight(n((D, U)) / fd[:, None], "e4m3")
    return {
        "query": (n((D, Q)) * 1.0 / np.sqrt(D) * fd[:, None]).astype(np.float32),
        "keys_words": keysp[0],
        "keys_scales": keysp[1],
        "notes_words": notesp[0],
        "notes_scales": notesp[1],
        "thr": (np.random.uniform(-0.6, 0.6, (Q, 1))).astype(np.float32),
        "slope": (np.random.uniform(1.0, 3.0, (Q, 1))).astype(np.float32),
        "offs": striped8(idx),
        "offs2": striped8(idx2),
        "offs3": striped8(idx3),
        "offs4": striped8(idx4),
    }


def reference(query, keys_words, keys_scales, notes_words, notes_scales, thr, slope, offs, offs2, offs3, offs4):
    idx = unstriped8(offs)
    idx2 = unstriped8(offs2)
    idx3 = unstriped8(offs3)
    idx4 = unstriped8(offs4)
    keysu = unpack_weight(keys_words, keys_scales, "e2m1")
    notesu = unpack_weight(notes_words, notes_scales, "e4m3")
    queryq = mxq(f64(query), 0, "e4m3")
    a = queryq.T @ keysu
    b = queryq.T @ notesu
    s2 = sigmoid(pick8(b, idx2, 16) * f64(slope) + f64(thr))
    f1 = np.zeros((Q, T))
    f1[np.arange(Q)[:, None], idx[np.arange(Q) % 128 // 16]] = s2
    cc = a - f1 * 2.0
    y = np.maximum(pick8(cc, idx3, 16), pick8(cc, idx4, 16))
    return y

@@ -1,0 +1,122 @@
+from contextlib import ExitStack
+
+import concourse.mybir as mybir
+
+F32 = mybir.dt.float32
+BF16 = mybir.dt.bfloat16
+I32 = mybir.dt.int32
+U32 = mybir.dt.uint32
+U16 = mybir.dt.uint16
+U8 = mybir.dt.uint8
+FP8X4 = mybir.dt.float8_e4m3fn_x4
+FP4X4 = mybir.dt.float4_e2m1fn_x4
+ALU = mybir.AluOpType
+ACT = mybir.ActivationFunctionType
+
+P = 128
+PACK = 4
+D, T, U, SLOTS, Q = 512, 1024, 1024, 512, 128
+BANK = 512
+NOTE_PASS = 256
+PIECE = 256
+LIST_COLS = PIECE // 16
+
+FLOPS = 2 * D * Q * (T + U)
+
+
+def load_scale_rows(queue, plane, scales):
+    for r in range(PACK):
+        queue.dma_start(out=plane[r:P:32, :].bitcast(I32), in_=scales[0, r:16:PACK, :].bitcast(I32))
+
+
+def tile_attend_guarded_two_kernel(tc, query, keys_words, keys_scales, notes_words, notes_scales,
+                                    thr, slope, offs, offs2, offs3, offs4, out):
+    nc = tc.nc
+    with ExitStack() as ctx:
+        lists = ctx.enter_context(tc.tile_pool(name="lists", bufs=1))
+        pool = ctx.enter_context(tc.tile_pool(name="pool", bufs=1))
+        psum = ctx.enter_context(tc.psum_pool(name="psum", bufs=1))
+
+        note_plane = pool.tile([P, U], U8, align_bytes=64)
+        key_plane = pool.tile([P, T], U8, align_bytes=64)
+        f1 = pool.tile([P, T], F32)
+        nc.vector.memset(note_plane[:].bitcast(I32), 0)
+        nc.vector.memset(key_plane[:].bitcast(I32), 0)
+        nc.vector.memset(f1[:], 0.0)
+
+        q_raw = pool.tile([P, PACK, Q], F32)
+        nc.sync.dma_start(out=q_raw[:], in_=query.rearrange("(p j) q -> p j q", j=PACK))
+        notes_flat = notes_words[0].rearrange("p u r -> p (u r)")
+        note_codes = []
+        for h in range(U // BANK):
+            codes = pool.tile([P, BANK], U32, name="note_codes%d" % h, align_bytes=64)
+            nc.sync.dma_start(out=codes[:].bitcast(I32),
+                              in_=notes_flat[:, h * BANK * PACK:(h + 1) * BANK * PACK].bitcast(I32))
+            note_codes.append(codes)
+        load_scale_rows(nc.scalar, note_plane, notes_scales)
+        slope_col = pool.tile([P, 1], F32)
+        thr_col = pool.tile([P, 1], F32)
+        nc.gpsimd.dma_start(out=slope_col[:], in_=slope)
+        nc.gpsimd.dma_start(out=thr_col[:], in_=thr)
+
+        note_list = lists.tile([P, SLOTS // 16], U16)
+        place_list = lists.tile([P, SLOTS // 16], U16)
+        first_list = lists.tile([P, SLOTS // 16], U16)
+        second_list = lists.tile([P, SLOTS // 16], U16)
+        nc.sync.dma_start(note_list[:], offs2)
+        nc.sync.dma_start(place_list[:], offs)
+        key_codes = pool.tile([P, 2 * T], U8, align_bytes=64)
+        nc.sync.dma_start(out=key_codes[:].bitcast(I32), in_=keys_words[0].bitcast(I32))
+        load_scale_rows(nc.sync, key_plane, keys_scales)
+        nc.sync.dma_start(first_list[:], offs3)
+        nc.sync.dma_start(second_list[:], offs4)
+
+        q_grouped = pool.tile([P, Q, PACK], BF16, align_bytes=64)
+        nc.vector.tensor_copy(out=q_grouped[:].rearrange("p (c i) j -> p c j i", i=4),
+                              in_=q_raw[:].rearrange("p j (c i) -> p c j i", i=4))
+        q_codes = pool.tile([P, Q], U32, align_bytes=64)
+        q_plane = pool.tile([P, Q], U8, align_bytes=64)
+        nc.vector.quantize_mx(out=q_codes[:].bitcast(FP8X4), scales=q_plane[:],
+                              in_=q_grouped[:].rearrange("p q j -> p (q j)"))
+
+        b = pool.tile([P, U], F32)
+        for n in range(U // NOTE_PASS):
+            c0 = n * NOTE_PASS
+            bank = psum.tile([P, NOTE_PASS], F32, name="b_bank%d" % n)
+            nc.tensor.matmul_mx(out=bank[:], lhsT=q_codes[:].bitcast(FP8X4), lhsT_scale=q_plane[:],
+                                rhs=note_codes[c0 // BANK][:, c0 % BANK:c0 % BANK + NOTE_PASS].bitcast(FP8X4),
+                                rhs_scale=note_plane[:, c0:c0 + NOTE_PASS], start=True, stop=True)
+            nc.vector.tensor_copy(out=b[:, c0:c0 + NOTE_PASS], in_=bank[:])
+
+        a_banks = []
+        for n in range(T // BANK):
+            c0 = n * BANK
+            bank = psum.tile([P, BANK], F32, name="a_bank%d" % n)
+            nc.tensor.matmul_mx(out=bank[:], lhsT=q_codes[:].bitcast(FP8X4), lhsT_scale=q_plane[:],
+                                rhs=key_codes[:, 2 * c0:2 * (c0 + BANK)].bitcast(FP4X4),
+                                rhs_scale=key_plane[:, c0:c0 + BANK], start=True, stop=True)
+            a_banks.append(bank)
+
+        pieces = SLOTS // PIECE
+        for h in range(pieces):
+            cols = slice(h * LIST_COLS, (h + 1) * LIST_COLS)
+            s2 = pool.tile([P, PIECE], F32, name="s2_%d" % h)
+            nc.scalar.activation(out=s2[:], in_=b[:].indirect(note_list[:, cols]), func=ACT.Sigmoid,
+                                 bias=thr_col[:], scale=slope_col[:])
+            nc.vector.tensor_copy(out=f1[:].indirect(place_list[:, cols]), in_=s2[:])
+
+        cc = pool.tile([P, T], F32)
+        for n in range(T // BANK):
+            c = slice(n * BANK, (n + 1) * BANK)
+            nc.vector.scalar_tensor_tensor(out=cc[:, c], in0=f1[:, c], scalar=-2.0, in1=a_banks[n][:],
+                                           op0=ALU.mult, op1=ALU.add)
+
+        for h in range(pieces):
+            cols = slice(h * LIST_COLS, (h + 1) * LIST_COLS)
+            first = pool.tile([P, PIECE], F32, name="first%d" % h)
+            second = pool.tile([P, PIECE], F32, name="second%d" % h)
+            larger = pool.tile([P, PIECE], F32, name="larger%d" % h)
+            nc.vector.tensor_copy(out=first[:], in_=cc[:].indirect(first_list[:, cols]))
+            nc.scalar.activation(out=second[:], in_=cc[:].indirect(second_list[:, cols]), func=ACT.Copy)
+            nc.vector.tensor_tensor(out=larger[:], in0=first[:], in1=second[:], op=ALU.max)
+            nc.sync.dma_start(out=out[:, h * PIECE:(h + 1) * PIECE], in_=larger[:])

@@ -40,12 +40,16 @@ def tile_attend_guarded_two_kernel(tc, query, keys_words, keys_scales, notes_wor
         note_plane = pool.tile([P, U], U8, align_bytes=64)
         key_plane = pool.tile([P, T], U8, align_bytes=64)
         f1 = pool.tile([P, T], F32)
-        nc.vector.memset(note_plane[:].bitcast(I32), 0)
-        nc.vector.memset(key_plane[:].bitcast(I32), 0)
+        warm_in = pool.tile([P, 1], F32)
+        warm_out = pool.tile([P, 1], F32)
+        nc.vector.memset(warm_in[:], 0.0)
         nc.vector.memset(f1[:], 0.0)
 
+        slope_col = pool.tile([P, 1], F32)
+        thr_col = pool.tile([P, 1], F32)
         q_raw = pool.tile([P, PACK, Q], F32)
         nc.sync.dma_start(out=q_raw[:], in_=query.rearrange("(p j) q -> p j q", j=PACK))
+        load_scale_rows(nc.sync, note_plane, notes_scales)
         notes_flat = notes_words[0].rearrange("p u r -> p (u r)")
         note_codes = []
         for h in range(U // BANK):
@@ -53,11 +57,9 @@ def tile_attend_guarded_two_kernel(tc, query, keys_words, keys_scales, notes_wor
             nc.sync.dma_start(out=codes[:].bitcast(I32),
                               in_=notes_flat[:, h * BANK * PACK:(h + 1) * BANK * PACK].bitcast(I32))
             note_codes.append(codes)
-        load_scale_rows(nc.scalar, note_plane, notes_scales)
-        slope_col = pool.tile([P, 1], F32)
-        thr_col = pool.tile([P, 1], F32)
-        nc.gpsimd.dma_start(out=slope_col[:], in_=slope)
-        nc.gpsimd.dma_start(out=thr_col[:], in_=thr)
+        nc.sync.dma_start(out=thr_col[:], in_=thr)
+        nc.sync.dma_start(out=slope_col[:], in_=slope)
+        nc.scalar.activation(out=warm_out[:], in_=warm_in[:], func=ACT.Sigmoid)
 
         note_list = lists.tile([P, SLOTS // 16], U16)
         place_list = lists.tile([P, SLOTS // 16], U16)
@@ -72,12 +74,15 @@ def tile_attend_guarded_two_kernel(tc, query, keys_words, keys_scales, notes_wor
         nc.sync.dma_start(second_list[:], offs4)
 
         q_grouped = pool.tile([P, Q, PACK], BF16, align_bytes=64)
-        nc.vector.tensor_copy(out=q_grouped[:].rearrange("p (c i) j -> p c j i", i=4),
-                              in_=q_raw[:].rearrange("p j (c i) -> p c j i", i=4))
         q_codes = pool.tile([P, Q], U32, align_bytes=64)
         q_plane = pool.tile([P, Q], U8, align_bytes=64)
-        nc.vector.quantize_mx(out=q_codes[:].bitcast(FP8X4), scales=q_plane[:],
-                              in_=q_grouped[:].rearrange("p q j -> p (q j)"))
+        halves = [slice(0, Q // 2), slice(Q // 2, Q)]
+        for rows in halves:
+            nc.vector.tensor_copy(out=q_grouped[:, rows, :].rearrange("p (c i) j -> p c j i", i=4),
+                                  in_=q_raw[:, :, rows].rearrange("p j (c i) -> p c j i", i=4))
+        for rows in halves:
+            nc.vector.quantize_mx(out=q_codes[:, rows].bitcast(FP8X4), scales=q_plane[:, rows],
+                                  in_=q_grouped[:, rows, :].rearrange("p q j -> p (q j)"))
 
         b = pool.tile([P, U], F32)
         for n in range(U // NOTE_PASS):
@@ -86,7 +91,10 @@ def tile_attend_guarded_two_kernel(tc, query, keys_words, keys_scales, notes_wor
             nc.tensor.matmul_mx(out=bank[:], lhsT=q_codes[:].bitcast(FP8X4), lhsT_scale=q_plane[:],
                                 rhs=note_codes[c0 // BANK][:, c0 % BANK:c0 % BANK + NOTE_PASS].bitcast(FP8X4),
                                 rhs_scale=note_plane[:, c0:c0 + NOTE_PASS], start=True, stop=True)
-            nc.vector.tensor_copy(out=b[:, c0:c0 + NOTE_PASS], in_=bank[:])
+            if n % 2 == 0:
+                nc.scalar.copy(out=b[:, c0:c0 + NOTE_PASS], in_=bank[:])
+            else:
+                nc.vector.tensor_copy(out=b[:, c0:c0 + NOTE_PASS], in_=bank[:])
 
         a_banks = []
         for n in range(T // BANK):

@@ -17,7 +17,8 @@ P = 128
 PACK = 4
 D, T, U, SLOTS, Q = 512, 1024, 1024, 512, 128
 BANK = 512
-NOTE_PASS = 256
+NOTE_PASSES = [(256, True), (256, False), (256, True), (128, False), (128, False)]
+KEY_PASSES = [(0, 512), (512, 256), (768, 256)]
 PIECE = 256
 LIST_COLS = PIECE // 16
 
@@ -85,24 +86,24 @@ def tile_attend_guarded_two_kernel(tc, query, keys_words, keys_scales, notes_wor
                                   in_=q_grouped[:, rows, :].rearrange("p q j -> p (q j)"))
 
         b = pool.tile([P, U], F32)
-        for n in range(U // NOTE_PASS):
-            c0 = n * NOTE_PASS
-            bank = psum.tile([P, NOTE_PASS], F32, name="b_bank%d" % n)
+        c0 = 0
+        for n, (width, on_scalar) in enumerate(NOTE_PASSES):
+            bank = psum.tile([P, width], F32, name="b_bank%d" % n)
             nc.tensor.matmul_mx(out=bank[:], lhsT=q_codes[:].bitcast(FP8X4), lhsT_scale=q_plane[:],
-                                rhs=note_codes[c0 // BANK][:, c0 % BANK:c0 % BANK + NOTE_PASS].bitcast(FP8X4),
-                                rhs_scale=note_plane[:, c0:c0 + NOTE_PASS], start=True, stop=True)
-            if n % 2 == 0:
-                nc.scalar.copy(out=b[:, c0:c0 + NOTE_PASS], in_=bank[:])
+                                rhs=note_codes[c0 // BANK][:, c0 % BANK:c0 % BANK + width].bitcast(FP8X4),
+                                rhs_scale=note_plane[:, c0:c0 + width], start=True, stop=True)
+            if on_scalar:
+                nc.scalar.copy(out=b[:, c0:c0 + width], in_=bank[:])
             else:
-                nc.vector.tensor_copy(out=b[:, c0:c0 + NOTE_PASS], in_=bank[:])
+                nc.vector.tensor_copy(out=b[:, c0:c0 + width], in_=bank[:])
+            c0 = c0 + width
 
         a_banks = []
-        for n in range(T // BANK):
-            c0 = n * BANK
-            bank = psum.tile([P, BANK], F32, name="a_bank%d" % n)
+        for c0, width in KEY_PASSES:
+            bank = psum.tile([P, width], F32, name="a_bank%d" % c0)
             nc.tensor.matmul_mx(out=bank[:], lhsT=q_codes[:].bitcast(FP8X4), lhsT_scale=q_plane[:],
-                                rhs=key_codes[:, 2 * c0:2 * (c0 + BANK)].bitcast(FP4X4),
-                                rhs_scale=key_plane[:, c0:c0 + BANK], start=True, stop=True)
+                                rhs=key_codes[:, 2 * c0:2 * (c0 + width)].bitcast(FP4X4),
+                                rhs_scale=key_plane[:, c0:c0 + width], start=True, stop=True)
             a_banks.append(bank)
 
         pieces = SLOTS // PIECE
@@ -111,13 +112,15 @@ def tile_attend_guarded_two_kernel(tc, query, keys_words, keys_scales, notes_wor
             s2 = pool.tile([P, PIECE], F32, name="s2_%d" % h)
             nc.scalar.activation(out=s2[:], in_=b[:].indirect(note_list[:, cols]), func=ACT.Sigmoid,
                                  bias=thr_col[:], scale=slope_col[:])
-            nc.vector.tensor_copy(out=f1[:].indirect(place_list[:, cols]), in_=s2[:])
+            nc.vector.tensor_tensor(out=f1[:].indirect(place_list[:, cols]), in0=s2[:], in1=s2[:], op=ALU.add)
 
         cc = pool.tile([P, T], F32)
-        for n in range(T // BANK):
-            c = slice(n * BANK, (n + 1) * BANK)
-            nc.vector.scalar_tensor_tensor(out=cc[:, c], in0=f1[:, c], scalar=-2.0, in1=a_banks[n][:],
-                                           op0=ALU.mult, op1=ALU.add)
+        tail0, tail_width = KEY_PASSES[-1]
+        a_tail = pool.tile([P, tail_width], F32)
+        nc.scalar.copy(out=a_tail[:], in_=a_banks[-1][:])
+        nc.gpsimd.tensor_tensor(out=cc[:, tail0:], in0=a_tail[:], in1=f1[:, tail0:], op=ALU.subtract)
+        for (c0, width), bank in zip(KEY_PASSES[:-1], a_banks):
+            nc.vector.tensor_tensor(out=cc[:, c0:c0 + width], in0=bank[:], in1=f1[:, c0:c0 + width], op=ALU.subtract)
 
         for h in range(pieces):
             cols = slice(h * LIST_COLS, (h + 1) * LIST_COLS)

from contextlib import ExitStack

import concourse.mybir as mybir

F32 = mybir.dt.float32
BF16 = mybir.dt.bfloat16
I32 = mybir.dt.int32
U32 = mybir.dt.uint32
U16 = mybir.dt.uint16
U8 = mybir.dt.uint8
FP8X4 = mybir.dt.float8_e4m3fn_x4
FP4X4 = mybir.dt.float4_e2m1fn_x4
ALU = mybir.AluOpType
ACT = mybir.ActivationFunctionType

P = 128
PACK = 4
D, T, U, SLOTS, Q = 512, 1024, 1024, 512, 128
BANK = 512
NOTE_PASSES = [(256, True), (256, False), (256, True), (128, False), (128, False)]
KEY_PASSES = [(0, 512), (512, 256), (768, 256)]
PIECE = 256
LIST_COLS = PIECE // 16

FLOPS = 2 * D * Q * (T + U)


def load_scale_rows(queue, plane, scales):
    for r in range(PACK):
        queue.dma_start(out=plane[r:P:32, :].bitcast(I32), in_=scales[0, r:16:PACK, :].bitcast(I32))


def tile_attend_guarded_two_kernel(tc, query, keys_words, keys_scales, notes_words, notes_scales,
                                    thr, slope, offs, offs2, offs3, offs4, out):
    nc = tc.nc
    with ExitStack() as ctx:
        lists = ctx.enter_context(tc.tile_pool(name="lists", bufs=1))
        pool = ctx.enter_context(tc.tile_pool(name="pool", bufs=1))
        psum = ctx.enter_context(tc.psum_pool(name="psum", bufs=1))

        note_plane = pool.tile([P, U], U8, align_bytes=64)
        key_plane = pool.tile([P, T], U8, align_bytes=64)
        f1 = pool.tile([P, T], F32)
        warm_in = pool.tile([P, 1], F32)
        warm_out = pool.tile([P, 1], F32)
        nc.vector.memset(warm_in[:], 0.0)
        nc.vector.memset(f1[:], 0.0)

        slope_col = pool.tile([P, 1], F32)
        thr_col = pool.tile([P, 1], F32)
        q_raw = pool.tile([P, PACK, Q], F32)
        nc.sync.dma_start(out=q_raw[:], in_=query.rearrange("(p j) q -> p j q", j=PACK))
        load_scale_rows(nc.sync, note_plane, notes_scales)
        notes_flat = notes_words[0].rearrange("p u r -> p (u r)")
        note_codes = []
        for h in range(U // BANK):
            codes = pool.tile([P, BANK], U32, name="note_codes%d" % h, align_bytes=64)
            nc.sync.dma_start(out=codes[:].bitcast(I32),
                              in_=notes_flat[:, h * BANK * PACK:(h + 1) * BANK * PACK].bitcast(I32))
            note_codes.append(codes)
        nc.sync.dma_start(out=thr_col[:], in_=thr)
        nc.sync.dma_start(out=slope_col[:], in_=slope)
        nc.scalar.activation(out=warm_out[:], in_=warm_in[:], func=ACT.Sigmoid)

        note_list = lists.tile([P, SLOTS // 16], U16)
        place_list = lists.tile([P, SLOTS // 16], U16)
        first_list = lists.tile([P, SLOTS // 16], U16)
        second_list = lists.tile([P, SLOTS // 16], U16)
        nc.sync.dma_start(note_list[:], offs2)
        nc.sync.dma_start(place_list[:], offs)
        key_codes = pool.tile([P, 2 * T], U8, align_bytes=64)
        nc.sync.dma_start(out=key_codes[:].bitcast(I32), in_=keys_words[0].bitcast(I32))
        load_scale_rows(nc.sync, key_plane, keys_scales)
        nc.sync.dma_start(first_list[:], offs3)
        nc.sync.dma_start(second_list[:], offs4)

        q_grouped = pool.tile([P, Q, PACK], BF16, align_bytes=64)
        q_codes = pool.tile([P, Q], U32, align_bytes=64)
        q_plane = pool.tile([P, Q], U8, align_bytes=64)
        halves = [slice(0, Q // 2), slice(Q // 2, Q)]
        for rows in halves:
            nc.vector.tensor_copy(out=q_grouped[:, rows, :].rearrange("p (c i) j -> p c j i", i=4),
                                  in_=q_raw[:, :, rows].rearrange("p j (c i) -> p c j i", i=4))
        for rows in halves:
            nc.vector.quantize_mx(out=q_codes[:, rows].bitcast(FP8X4), scales=q_plane[:, rows],
                                  in_=q_grouped[:, rows, :].rearrange("p q j -> p (q j)"))

        b = pool.tile([P, U], F32)
        c0 = 0
        for n, (width, on_scalar) in enumerate(NOTE_PASSES):
            bank = psum.tile([P, width], F32, name="b_bank%d" % n)
            nc.tensor.matmul_mx(out=bank[:], lhsT=q_codes[:].bitcast(FP8X4), lhsT_scale=q_plane[:],
                                rhs=note_codes[c0 // BANK][:, c0 % BANK:c0 % BANK + width].bitcast(FP8X4),
                                rhs_scale=note_plane[:, c0:c0 + width], start=True, stop=True)
            if on_scalar:
                nc.scalar.copy(out=b[:, c0:c0 + width], in_=bank[:])
            else:
                nc.vector.tensor_copy(out=b[:, c0:c0 + width], in_=bank[:])
            c0 = c0 + width

        a_banks = []
        for c0, width in KEY_PASSES:
            bank = psum.tile([P, width], F32, name="a_bank%d" % c0)
            nc.tensor.matmul_mx(out=bank[:], lhsT=q_codes[:].bitcast(FP8X4), lhsT_scale=q_plane[:],
                                rhs=key_codes[:, 2 * c0:2 * (c0 + width)].bitcast(FP4X4),
                                rhs_scale=key_plane[:, c0:c0 + width], start=True, stop=True)
            a_banks.append(bank)

        pieces = SLOTS // PIECE
        for h in range(pieces):
            cols = slice(h * LIST_COLS, (h + 1) * LIST_COLS)
            s2 = pool.tile([P, PIECE], F32, name="s2_%d" % h)
            nc.scalar.activation(out=s2[:], in_=b[:].indirect(note_list[:, cols]), func=ACT.Sigmoid,
                                 bias=thr_col[:], scale=slope_col[:])
            nc.vector.tensor_tensor(out=f1[:].indirect(place_list[:, cols]), in0=s2[:], in1=s2[:], op=ALU.add)

        cc = pool.tile([P, T], F32)
        tail0, tail_width = KEY_PASSES[-1]
        a_tail = pool.tile([P, tail_width], F32)
        nc.scalar.copy(out=a_tail[:], in_=a_banks[-1][:])
        nc.gpsimd.tensor_tensor(out=cc[:, tail0:], in0=a_tail[:], in1=f1[:, tail0:], op=ALU.subtract)
        for (c0, width), bank in zip(KEY_PASSES[:-1], a_banks):
            nc.vector.tensor_tensor(out=cc[:, c0:c0 + width], in0=bank[:], in1=f1[:, c0:c0 + width], op=ALU.subtract)

        for h in range(pieces):
            cols = slice(h * LIST_COLS, (h + 1) * LIST_COLS)
            first = pool.tile([P, PIECE], F32, name="first%d" % h)
            second = pool.tile([P, PIECE], F32, name="second%d" % h)
            larger = pool.tile([P, PIECE], F32, name="larger%d" % h)
            nc.vector.tensor_copy(out=first[:], in_=cc[:].indirect(first_list[:, cols]))
            nc.scalar.activation(out=second[:], in_=cc[:].indirect(second_list[:, cols]), func=ACT.Copy)
            nc.vector.tensor_tensor(out=larger[:], in0=first[:], in1=second[:], op=ALU.max)
            nc.sync.dma_start(out=out[:, h * PIECE:(h + 1) * PIECE], in_=larger[:])
